import numpy as np
import ml_dtypes


def mxq(x, axis, fmt="e4m3"):
    dtype, down = {"e4m3": (ml_dtypes.float8_e4m3fn, 7), "e5m2": (ml_dtypes.float8_e5m2, 14)}[fmt]
    v = np.moveaxis(np.asarray(x, np.float32).astype(ml_dtypes.bfloat16).astype(np.float64), axis, -1)
    blocks = v.reshape(v.shape[:-1] + (-1, 32))
    amax = np.abs(blocks).max(-1, keepdims=True)
    byte = np.maximum(np.where(amax > 0, np.frexp(amax)[1] - 1 + 127, 0) - down, 1)
    scale = np.exp2(byte - 127.0)
    codes = (blocks / scale).astype(np.float32).astype(dtype).astype(np.float64)
    return np.moveaxis((codes * scale).reshape(v.shape), -1, axis)


WIDE = False


def mx_kscale(k):
    if not WIDE:
        return np.ones(k)
    levels = np.array([10, -10, 5, -5, 0])
    if k % 512:
        return np.exp2(np.random.permutation(np.resize(levels, k // 32))).repeat(32)
    a = np.empty((k // 512, 16))
    for p in range(k // 512):
        a[p, :8] = np.random.permutation(np.resize(levels, 8))
        for g in range(8):
            far = levels[np.abs(levels - a[p, g]) >= 10]
            a[p, g + 8] = far[np.random.randint(len(far))]
    return np.exp2(a.ravel()).repeat(32)


def f64(x):
    return np.asarray(x).astype(np.float64)


def striped(idx):
    return np.tile(np.asarray(idx).reshape(-1, 16).T, (8, 1)).astype(np.uint16)


def unstriped(offs):
    return offs[:16].T.reshape(-1).astype(np.int64)


E2M1 = np.array([0.0, 0.5, 1.0, 1.5, 2.0, 3.0, 4.0, 6.0, -0.0, -0.5, -1.0, -1.5, -2.0, -3.0, -4.0, -6.0])


def pack_weight(w, fmt):
    k, n = w.shape
    w = f64(np.asarray(w, np.float32).astype(ml_dtypes.bfloat16)).reshape(k // 32, 32, n)
    amax = np.abs(w).max(1)
    if fmt == "e4m3":
        byte = np.frexp(amax)[1] - 1 + 127 - 7
    else:
        mant, ex = np.frexp(amax / 6.0)
        byte = np.where(mant > 0.5, ex, ex - 1) + 127
    byte = np.clip(np.where(amax > 0, byte, 1), 1, 254)
    scaled = (w * np.exp2(127.0 - byte)[:, None, :]).reshape(k, n).astype(np.float32)
    by_word = np.ascontiguousarray(scaled.reshape(k // 512, 128, 4, n).transpose(0, 1, 3, 2))
    if fmt == "e4m3":
        words = by_word.astype(ml_dtypes.float8_e4m3fn).view(np.uint8)
    else:
        c = by_word.astype(ml_dtypes.float4_e2m1fn).view(np.uint8) & 0xF
        words = (c[..., 0::2] | (c[..., 1::2] << 4)).reshape(k // 512, 128, 2 * n)
    return np.ascontiguousarray(words), np.ascontiguousarray(byte.astype(np.uint8).reshape(k // 512, 16, n))


def unpack_weight(words, scales, fmt):
    g, _, n = scales.shape
    words = np.ascontiguousarray(words).reshape(g, 128, n, -1)
    if fmt == "e4m3":
        vals = words.view(ml_dtypes.float8_e4m3fn).astype(np.float64)
    else:
        nib = np.empty((g, 128, n, 4), np.uint8)
        nib[..., 0::2] = words & 0xF
        nib[..., 1::2] = words >> 4
        vals = E2M1[nib]
    vals = vals * np.repeat(np.exp2(scales.astype(np.float64) - 127.0), 8, axis=1)[..., None]
    return vals.transpose(0, 1, 3, 2).reshape(g * 512, n)


D, E, T, I, Q = 512, 512, 2048, 512, 128


def setup_inputs():
    n = np.random.standard_normal
    idx = np.random.permutation(T)[:I]
    fd = mx_kscale(D)
    fe = mx_kscale(E)
    keysp = pack_weight(n((D, T)) / fd[:, None], "e4m3")
    valsp = pack_weight(n((E, T)) / fe[:, None], "e4m3")
    return {
        "query": (n((D, Q)) * 0.4 / np.sqrt(D) * fd[:, None]).astype(np.float32),
        "query2": (n((D, Q)) * 0.6 / np.sqrt(D) * fd[:, None]).astype(np.float32),
        "keys_words": keysp[0],
        "keys_scales": keysp[1],
        "l1": (np.random.uniform(6.2, 6.5, (Q, 1))).astype(np.float32),
        "l2": (np.random.uniform(6.2, 6.5, (Q, 1))).astype(np.float32),
        "floor": (np.random.uniform(0.0005, 0.002, (Q, 1))).astype(np.float32),
        "gout": (n((E, Q)) * 1 / np.sqrt(E) * fe[:, None]).astype(np.float32),
        "vals_words": valsp[0],
        "vals_scales": valsp[1],
        "size": (np.random.uniform(0.5, 2.0, (1, I))).astype(np.float32),
        "base": (0.5 * n((Q, I))).astype(np.float32),
        "offs": striped(idx),
    }


def reference(query, query2, keys_words, keys_scales, l1, l2, floor, gout, vals_words, vals_scales, size, base, offs):
    idx = unstriped(offs)
    keysu = unpack_weight(keys_words, keys_scales, "e4m3")
    valsu = unpack_weight(vals_words, vals_scales, "e4m3")
    queryq = mxq(f64(query), 0, "e4m3")
    keysidxg = keysu[:, idx]
    a = queryq.T @ keysidxg
    query2q = mxq(f64(query2), 0, "e4m3")
    b = query2q.T @ keysidxg
    pa = np.exp(a - f64(l1))
    pb = np.exp(b - f64(l2))
    goutq = mxq(f64(gout), 0, "e4m3")
    valsidxg = valsu[:, idx]
    c0 = goutq.T @ valsidxg
    dpb = c0 * f64(size) * pa / np.square(pb + f64(floor)) * (-1.0)
    db = dpb * pb
    hdb = db * 4.0 * 2.0 * 4.0
    hdpb = hdb * pb
    hpb = hdb * dpb + hdpb * (-1.0) * c0 * f64(size) * pa / np.square(np.square(pb + f64(floor))) * (-1.0) * (pb + f64(floor)) * 2.0
    hb = hpb * pb
    y = hb + f64(base)
    return y

@@ -1,0 +1,181 @@
+import concourse.mybir as mybir
+from concourse.masks import make_identity
+
+F32 = mybir.dt.float32
+BF16 = mybir.dt.bfloat16
+I32 = mybir.dt.int32
+U32 = mybir.dt.uint32
+U16 = mybir.dt.uint16
+U8 = mybir.dt.uint8
+FP8X4 = mybir.dt.float8_e4m3fn_x4
+ACT = mybir.ActivationFunctionType
+ALU = mybir.AluOpType
+
+P = 128
+PACK = 4
+D, T, SLOTS, Q = 512, 2048, 512, 128
+HALVES = 2
+HALF = SLOTS // HALVES
+VAL_ROW = 4
+
+FLOPS = 3 * 2 * D * Q * SLOTS
+
+
+def tile_attend_gpclippedratio_b_kernel(
+    tc, query, query2, keys_words, keys_scales, l1, l2, floor, gout, vals_words, vals_scales, size, base, offs, out
+):
+    nc = tc.nc
+    with (
+        tc.tile_pool(name="held", bufs=1) as held,
+        tc.psum_pool(name="psum", bufs=1) as psum,
+    ):
+        offsets = held.tile([P, SLOTS // 16], U16, name="offsets")
+        key_words = held.tile([P, T], U32, name="key_words")
+        val_words = held.tile([P, T], U32, name="val_words")
+        key_scales = held.tile([P, T], U8, name="key_scales")
+        val_scales = held.tile([P, T], U8, name="val_scales")
+        raw = {n: held.tile([P, PACK, Q], F32, name="raw_" + n) for n in ("q2", "q", "g")}
+        floor_col = held.tile([P, 1], F32, name="floor_col")
+        l1_col = held.tile([P, 1], F32, name="l1_col")
+        l2_col = held.tile([P, 1], F32, name="l2_col")
+        size_cols = held.tile([P, PACK], F32, name="size_cols")
+        base_sb = held.tile([P, SLOTS], F32, name="base_sb")
+
+        nc.vector.memset(key_scales[:].bitcast(I32), 0)
+        nc.vector.memset(val_scales[:].bitcast(I32), 0)
+
+        def load_rows(name, src):
+            nc.sync.dma_start(out=raw[name][:], in_=src.rearrange("(p j) w -> p j w", j=PACK))
+
+        def load_words(dst, src):
+            nc.sync.dma_start(out=dst[:].bitcast(I32), in_=src[0].rearrange("p n t -> p (n t)").bitcast(I32))
+
+        def load_scales(dst, src, first_row):
+            for quad in range(4):
+                nc.sync.dma_start(
+                    out=dst[32 * quad + first_row : 32 * quad + first_row + 4, :].bitcast(I32),
+                    in_=src[0, 4 * quad : 4 * quad + 4, :].bitcast(I32),
+                )
+
+        load_rows("q2", query2)
+        nc.sync.dma_start(offsets[:], offs)
+        nc.sync.dma_start(out=floor_col[:], in_=floor)
+        load_scales(key_scales, keys_scales, 0)
+        load_words(key_words, keys_words)
+        load_scales(val_scales, vals_scales, VAL_ROW)
+        load_rows("q", query)
+        load_rows("g", gout)
+        load_words(val_words, vals_words)
+        nc.sync.dma_start(out=base_sb[:], in_=base)
+        nc.gpsimd.dma_start(out=l2_col[:], in_=l2)
+        nc.gpsimd.dma_start(out=l1_col[:], in_=l1)
+        nc.gpsimd.dma_start(out=size_cols[:], in_=size[0].rearrange("(p j) -> p j", j=PACK))
+
+        ident = held.tile([P, P], F32, name="ident")
+        make_identity(nc, ident[:])
+
+        ln_floor = held.tile([P, 1], F32, name="ln_floor")
+        nc.scalar.activation(out=ln_floor[:], in_=floor_col[:], func=ACT.Ln)
+        sig_bias = held.tile([P, 1], F32, name="sig_bias")
+        nc.gpsimd.tensor_scalar(sig_bias[:], ln_floor[:], 1.0, l2_col[:], ALU.mult, ALU.add)
+        neg_sig_bias = held.tile([P, 1], F32, name="neg_sig_bias")
+        nc.gpsimd.tensor_scalar(neg_sig_bias[:], ln_floor[:], l2_col[:], -1.0, ALU.add, ALU.mult)
+        exp_bias = held.tile([P, 1], F32, name="exp_bias")
+        nc.gpsimd.tensor_scalar(exp_bias[:], ln_floor[:], l1_col[:], -1.0, ALU.add, ALU.mult)
+
+        codes, planes = {}, {}
+
+        def quantise(name):
+            grouped = held.tile([P, Q, PACK], BF16, name="grouped_" + name, align_bytes=64)
+            nc.scalar.copy(
+                out=grouped[:].rearrange("p (c i) t -> p c t i", i=4),
+                in_=raw[name][:].rearrange("p t (c i) -> p c t i", i=4),
+            )
+            codes[name] = held.tile([P, Q], U32, name="codes_" + name, align_bytes=64)
+            planes[name] = held.tile([P, Q], U8, name="plane_" + name, align_bytes=64)
+            nc.vector.quantize_mx(
+                out=codes[name][:].bitcast(FP8X4), scales=planes[name][:], in_=grouped[:].rearrange("p w j -> p (w j)")
+            )
+
+        def gather(name, window, dtype, lists):
+            picked = held.tile([P, lists.shape[1] * 16], dtype, name=name, align_bytes=64)
+            nc.vector.tensor_copy(picked[:], window[:].indirect(lists))
+            return picked
+
+        def half_list(h):
+            return offsets[:, h * HALF // 16 : (h + 1) * HALF // 16]
+
+        def cols(h):
+            return slice(h * HALF, (h + 1) * HALF)
+
+        key_scales_g = gather("key_scales_g", key_scales, U8, offsets[:])
+        quantise("q2")
+        key_g = [gather("key_g%d" % h, key_words, U32, half_list(h)) for h in range(HALVES)]
+
+        size_bank = psum.tile([P, PACK, P], F32, name="size_bank")
+        for j in range(PACK):
+            nc.tensor.transpose(size_bank[:, j, :], size_cols[:, j : j + 1].to_broadcast([P, P]), ident[:])
+
+        score = [psum.tile([P, HALF], F32, name="score%d" % h) for h in range(HALVES)]
+        share = [held.tile([P, HALF], F32, name="share%d" % h) for h in range(HALVES)]
+        rest = [held.tile([P, HALF], F32, name="rest%d" % h) for h in range(HALVES)]
+        score_a = [psum.tile([P, HALF], F32, name="score_a%d" % h) for h in range(HALVES)]
+        share_sq = [held.tile([P, HALF], F32, name="share_sq%d" % h) for h in range(HALVES)]
+
+        def product(bank, name, words, scales, start):
+            nc.tensor.matmul_mx(
+                out=bank[:],
+                lhsT=codes[name][:].bitcast(FP8X4),
+                lhsT_scale=planes[name][:],
+                rhs=words[:].bitcast(FP8X4),
+                rhs_scale=scales,
+                start=start,
+                stop=True,
+            )
+
+        for h in range(HALVES):
+            product(score[h], "q2", key_g[h], key_scales_g[:, cols(h)], True)
+            nc.scalar.activation(out=share[h][:], in_=score[h][:], func=ACT.Sigmoid, scale=-1.0, bias=sig_bias[:])
+            nc.scalar.activation(out=rest[h][:], in_=score[h][:], func=ACT.Sigmoid, bias=neg_sig_bias[:])
+
+        quantise("q")
+        quantise("g")
+        val_scales_g = gather("val_scales_g", val_scales, U8, offsets[:])
+
+        weight = []
+        for h in range(HALVES):
+            nc.vector.tensor_tensor(share_sq[h][:], share[h][:], rest[h][:], ALU.mult)
+            x = held.tile([P, HALF], F32, name="weight%d" % h)
+            n0 = h * HALF // PACK
+            nc.vector.tensor_tensor(
+                x[:].rearrange("p (n j) -> p n j", j=PACK),
+                size_bank[:, :, n0 : n0 + HALF // PACK].rearrange("p j n -> p n j"),
+                share_sq[h][:].rearrange("p (n j) -> p n j", j=PACK),
+                ALU.mult,
+            )
+            weight.append(x)
+
+        joint = []
+        for h in range(HALVES):
+            product(score_a[h], "q", key_g[h], key_scales_g[:, cols(h)], True)
+            e = held.tile([P, HALF], F32, name="joint%d" % h)
+            nc.scalar.activation(out=e[:], in_=score_a[h][:], func=ACT.Exp, bias=exp_bias[:])
+            joint.append(e)
+
+        val_g = [gather("val_g%d" % h, val_words, U32, half_list(h)) for h in range(HALVES)]
+        c0 = [psum.tile([P, HALF], F32, name="c0_%d" % h) for h in range(HALVES)]
+        xc, v, vsq, g, y = [
+            [held.tile([P, HALF], F32, name="%s%d" % (n, h)) for h in range(HALVES)]
+            for n in ("xc", "v", "vsq", "g", "y")
+        ]
+        for h in range(HALVES):
+            product(c0[h], "g", val_g[h], val_scales_g[VAL_ROW:P, cols(h)], True)
+            nc.vector.tensor_tensor(xc[h][:], c0[h][:], weight[h][:], ALU.mult)
+        for h in range(HALVES):
+            nc.vector.tensor_tensor(v[h][:], xc[h][:], joint[h][:], ALU.mult)
+            nc.scalar.activation(out=vsq[h][:], in_=v[h][:], func=ACT.Square)
+        for h in range(HALVES):
+            nc.vector.scalar_tensor_tensor(g[h][:], share[h][:], 0.5, vsq[h][:], ALU.subtract, ALU.mult)
+        for h in range(HALVES):
+            nc.vector.scalar_tensor_tensor(y[h][:], g[h][:], 64.0, base_sb[:, cols(h)], ALU.mult, ALU.add)
+            nc.sync.dma_start(out=out[:, cols(h)], in_=y[h][:])

@@ -31,17 +31,17 @@ def tile_attend_gpclippedratio_b_kernel(
     ):
         offsets = held.tile([P, SLOTS // 16], U16, name="offsets")
         key_words = held.tile([P, T], U32, name="key_words")
-        val_words = held.tile([P, T], U32, name="val_words")
+        val_words = held.tile([P, T], U32, name="val_words", tag="val_words")
         key_scales = held.tile([P, T], U8, name="key_scales")
         val_scales = held.tile([P, T], U8, name="val_scales")
-        raw = {n: held.tile([P, PACK, Q], F32, name="raw_" + n) for n in ("q2", "q", "g")}
+        raw = {n: held.tile([P, PACK, Q], F32, name="raw_" + n, tag="raw_" + n) for n in ("q2", "q", "g")}
         floor_col = held.tile([P, 1], F32, name="floor_col")
         l1_col = held.tile([P, 1], F32, name="l1_col")
         l2_col = held.tile([P, 1], F32, name="l2_col")
         size_cols = held.tile([P, PACK], F32, name="size_cols")
         base_sb = held.tile([P, SLOTS], F32, name="base_sb")
 
-        nc.vector.memset(key_scales[:].bitcast(I32), 0)
+        nc.gpsimd.memset(key_scales[:].bitcast(I32), 0)
         nc.vector.memset(val_scales[:].bitcast(I32), 0)
 
         def load_rows(name, src):
@@ -50,44 +50,48 @@ def tile_attend_gpclippedratio_b_kernel(
         def load_words(dst, src):
             nc.sync.dma_start(out=dst[:].bitcast(I32), in_=src[0].rearrange("p n t -> p (n t)").bitcast(I32))
 
-        def load_scales(dst, src, first_row):
+        def load_scales(queue, dst, src, first_row):
             for quad in range(4):
-                nc.sync.dma_start(
+                queue.dma_start(
                     out=dst[32 * quad + first_row : 32 * quad + first_row + 4, :].bitcast(I32),
                     in_=src[0, 4 * quad : 4 * quad + 4, :].bitcast(I32),
                 )
 
-        load_rows("q2", query2)
         nc.sync.dma_start(offsets[:], offs)
+        load_scales(nc.sync, key_scales, keys_scales, 0)
         nc.sync.dma_start(out=floor_col[:], in_=floor)
-        load_scales(key_scales, keys_scales, 0)
+        nc.sync.dma_start(out=size_cols[:], in_=size[0].rearrange("(p j) -> p j", j=PACK))
         load_words(key_words, keys_words)
-        load_scales(val_scales, vals_scales, VAL_ROW)
+        load_rows("q2", query2)
+        load_scales(nc.sync, val_scales, vals_scales, VAL_ROW)
         load_rows("q", query)
         load_rows("g", gout)
         load_words(val_words, vals_words)
         nc.sync.dma_start(out=base_sb[:], in_=base)
         nc.gpsimd.dma_start(out=l2_col[:], in_=l2)
         nc.gpsimd.dma_start(out=l1_col[:], in_=l1)
-        nc.gpsimd.dma_start(out=size_cols[:], in_=size[0].rearrange("(p j) -> p j", j=PACK))
 
         ident = held.tile([P, P], F32, name="ident")
         make_identity(nc, ident[:])
 
+        size_bank = psum.tile([P, PACK, P], F32, name="size_bank")
+        for j in range(PACK):
+            nc.tensor.transpose(size_bank[:, j, :], size_cols[:, j : j + 1].to_broadcast([P, P]), ident[:])
+
         ln_floor = held.tile([P, 1], F32, name="ln_floor")
         nc.scalar.activation(out=ln_floor[:], in_=floor_col[:], func=ACT.Ln)
+        warm = held.tile([P, 1], F32, name="warm")
+        nc.scalar.activation(out=warm[:], in_=ln_floor[:], func=ACT.Sigmoid)
         sig_bias = held.tile([P, 1], F32, name="sig_bias")
-        nc.gpsimd.tensor_scalar(sig_bias[:], ln_floor[:], 1.0, l2_col[:], ALU.mult, ALU.add)
-        neg_sig_bias = held.tile([P, 1], F32, name="neg_sig_bias")
-        nc.gpsimd.tensor_scalar(neg_sig_bias[:], ln_floor[:], l2_col[:], -1.0, ALU.add, ALU.mult)
-        exp_bias = held.tile([P, 1], F32, name="exp_bias")
-        nc.gpsimd.tensor_scalar(exp_bias[:], ln_floor[:], l1_col[:], -1.0, ALU.add, ALU.mult)
+        nc.scalar.activation(out=sig_bias[:], in_=ln_floor[:], func=ACT.Identity, bias=l2_col[:])
+        neg_sig_bias = held.tile([P, 1], F32, name="neg_sig_bias", tag="grouped_g", align_bytes=64)
+        nc.scalar.activation(out=neg_sig_bias[:], in_=sig_bias[:], func=ACT.Identity, scale=-1.0)
 
         codes, planes = {}, {}
 
-        def quantise(name):
-            grouped = held.tile([P, Q, PACK], BF16, name="grouped_" + name, align_bytes=64)
-            nc.scalar.copy(
+        def quantise(name, copy):
+            grouped = held.tile([P, Q, PACK], BF16, name="grouped_" + name, tag="grouped_" + name, align_bytes=64)
+            copy(
                 out=grouped[:].rearrange("p (c i) t -> p c t i", i=4),
                 in_=raw[name][:].rearrange("p t (c i) -> p c t i", i=4),
             )
@@ -108,59 +112,46 @@ def tile_attend_gpclippedratio_b_kernel(
         def cols(h):
             return slice(h * HALF, (h + 1) * HALF)
 
-        key_scales_g = gather("key_scales_g", key_scales, U8, offsets[:])
-        quantise("q2")
-        key_g = [gather("key_g%d" % h, key_words, U32, half_list(h)) for h in range(HALVES)]
-
-        size_bank = psum.tile([P, PACK, P], F32, name="size_bank")
-        for j in range(PACK):
-            nc.tensor.transpose(size_bank[:, j, :], size_cols[:, j : j + 1].to_broadcast([P, P]), ident[:])
-
-        score = [psum.tile([P, HALF], F32, name="score%d" % h) for h in range(HALVES)]
-        share = [held.tile([P, HALF], F32, name="share%d" % h) for h in range(HALVES)]
-        rest = [held.tile([P, HALF], F32, name="rest%d" % h) for h in range(HALVES)]
-        score_a = [psum.tile([P, HALF], F32, name="score_a%d" % h) for h in range(HALVES)]
-        share_sq = [held.tile([P, HALF], F32, name="share_sq%d" % h) for h in range(HALVES)]
-
-        def product(bank, name, words, scales, start):
+        def product(bank, name, words, scales):
             nc.tensor.matmul_mx(
                 out=bank[:],
                 lhsT=codes[name][:].bitcast(FP8X4),
                 lhsT_scale=planes[name][:],
                 rhs=words[:].bitcast(FP8X4),
                 rhs_scale=scales,
-                start=start,
+                start=True,
                 stop=True,
             )
 
-        for h in range(HALVES):
-            product(score[h], "q2", key_g[h], key_scales_g[:, cols(h)], True)
-            nc.scalar.activation(out=share[h][:], in_=score[h][:], func=ACT.Sigmoid, scale=-1.0, bias=sig_bias[:])
-            nc.scalar.activation(out=rest[h][:], in_=score[h][:], func=ACT.Sigmoid, bias=neg_sig_bias[:])
+        key_scales_g = gather("key_scales_g", key_scales, U8, offsets[:])
+        key_g = gather("key_g", key_words, U32, offsets[:])
+        quantise("q2", nc.scalar.copy)
+        score_b = psum.tile([P, SLOTS], F32, name="score_b")
+        product(score_b, "q2", key_g, key_scales_g[:])
+        share = held.tile([P, SLOTS], F32, name="share")
+        rest = held.tile([P, SLOTS], F32, name="rest")
+        nc.scalar.activation(out=share[:], in_=score_b[:], func=ACT.Sigmoid, scale=-1.0, bias=sig_bias[:])
+        nc.scalar.activation(out=rest[:], in_=score_b[:], func=ACT.Sigmoid, bias=neg_sig_bias[:])
 
-        quantise("q")
-        quantise("g")
         val_scales_g = gather("val_scales_g", val_scales, U8, offsets[:])
+        quantise("q", nc.vector.tensor_copy)
+        score_a = psum.tile([P, SLOTS], F32, name="score_a")
+        product(score_a, "q", key_g, key_scales_g[:])
+        exp_bias = held.tile([P, 1], F32, name="exp_bias")
+        nc.gpsimd.tensor_scalar(exp_bias[:], ln_floor[:], l1_col[:], -1.0, ALU.add, ALU.mult)
 
-        weight = []
-        for h in range(HALVES):
-            nc.vector.tensor_tensor(share_sq[h][:], share[h][:], rest[h][:], ALU.mult)
-            x = held.tile([P, HALF], F32, name="weight%d" % h)
-            n0 = h * HALF // PACK
-            nc.vector.tensor_tensor(
-                x[:].rearrange("p (n j) -> p n j", j=PACK),
-                size_bank[:, :, n0 : n0 + HALF // PACK].rearrange("p j n -> p n j"),
-                share_sq[h][:].rearrange("p (n j) -> p n j", j=PACK),
-                ALU.mult,
-            )
-            weight.append(x)
-
-        joint = []
-        for h in range(HALVES):
-            product(score_a[h], "q", key_g[h], key_scales_g[:, cols(h)], True)
-            e = held.tile([P, HALF], F32, name="joint%d" % h)
-            nc.scalar.activation(out=e[:], in_=score_a[h][:], func=ACT.Exp, bias=exp_bias[:])
-            joint.append(e)
+        both = held.tile([P, SLOTS], F32, name="both")
+        nc.vector.tensor_tensor(both[:], share[:], rest[:], ALU.mult)
+        weight = held.tile([P, SLOTS], F32, name="weight")
+        nc.vector.tensor_tensor(
+            weight[:].rearrange("p (n j) -> p n j", j=PACK),
+            size_bank[:].rearrange("p j n -> p n j"),
+            both[:].rearrange("p (n j) -> p n j", j=PACK),
+            ALU.mult,
+        )
+        quantise("g", nc.scalar.copy)
+        joint = held.tile([P, SLOTS], F32, name="joint", tag="raw_g")
+        nc.scalar.activation(out=joint[:], in_=score_a[:], func=ACT.Exp, bias=exp_bias[:])
 
         val_g = [gather("val_g%d" % h, val_words, U32, half_list(h)) for h in range(HALVES)]
         c0 = [psum.tile([P, HALF], F32, name="c0_%d" % h) for h in range(HALVES)]
@@ -169,13 +160,13 @@ def tile_attend_gpclippedratio_b_kernel(
             for n in ("xc", "v", "vsq", "g", "y")
         ]
         for h in range(HALVES):
-            product(c0[h], "g", val_g[h], val_scales_g[VAL_ROW:P, cols(h)], True)
-            nc.vector.tensor_tensor(xc[h][:], c0[h][:], weight[h][:], ALU.mult)
+            product(c0[h], "g", val_g[h], val_scales_g[VAL_ROW:P, cols(h)])
+            nc.vector.tensor_tensor(xc[h][:], c0[h][:], weight[:, cols(h)], ALU.mult)
         for h in range(HALVES):
-            nc.vector.tensor_tensor(v[h][:], xc[h][:], joint[h][:], ALU.mult)
+            nc.vector.tensor_tensor(v[h][:], xc[h][:], joint[:, cols(h)], ALU.mult)
             nc.scalar.activation(out=vsq[h][:], in_=v[h][:], func=ACT.Square)
         for h in range(HALVES):
-            nc.vector.scalar_tensor_tensor(g[h][:], share[h][:], 0.5, vsq[h][:], ALU.subtract, ALU.mult)
+            nc.vector.scalar_tensor_tensor(g[h][:], share[:, cols(h)], 0.5, vsq[h][:], ALU.subtract, ALU.mult)
         for h in range(HALVES):
             nc.vector.scalar_tensor_tensor(y[h][:], g[h][:], 64.0, base_sb[:, cols(h)], ALU.mult, ALU.add)
             nc.sync.dma_start(out=out[:, cols(h)], in_=y[h][:])

@@ -62,14 +62,14 @@ def tile_attend_gpclippedratio_b_kernel(
         nc.sync.dma_start(out=floor_col[:], in_=floor)
         nc.sync.dma_start(out=size_cols[:], in_=size[0].rearrange("(p j) -> p j", j=PACK))
         load_words(key_words, keys_words)
+        nc.sync.dma_start(out=l2_col[:], in_=l2)
         load_rows("q2", query2)
         load_scales(nc.sync, val_scales, vals_scales, VAL_ROW)
-        load_rows("q", query)
-        load_rows("g", gout)
         load_words(val_words, vals_words)
+        load_rows("g", gout)
+        load_rows("q", query)
+        nc.sync.dma_start(out=l1_col[:], in_=l1)
         nc.sync.dma_start(out=base_sb[:], in_=base)
-        nc.gpsimd.dma_start(out=l2_col[:], in_=l2)
-        nc.gpsimd.dma_start(out=l1_col[:], in_=l1)
 
         ident = held.tile([P, P], F32, name="ident")
         make_identity(nc, ident[:])
@@ -101,13 +101,10 @@ def tile_attend_gpclippedratio_b_kernel(
                 out=codes[name][:].bitcast(FP8X4), scales=planes[name][:], in_=grouped[:].rearrange("p w j -> p (w j)")
             )
 
-        def gather(name, window, dtype, lists):
-            picked = held.tile([P, lists.shape[1] * 16], dtype, name=name, align_bytes=64)
+        def gather(name, window, dtype, lists, tag=None):
+            picked = held.tile([P, lists.shape[1] * 16], dtype, name=name, tag=tag or name, align_bytes=64)
             nc.vector.tensor_copy(picked[:], window[:].indirect(lists))
             return picked
-
-        def half_list(h):
-            return offsets[:, h * HALF // 16 : (h + 1) * HALF // 16]
 
         def cols(h):
             return slice(h * HALF, (h + 1) * HALF)
@@ -133,16 +130,17 @@ def tile_attend_gpclippedratio_b_kernel(
         nc.scalar.activation(out=share[:], in_=score_b[:], func=ACT.Sigmoid, scale=-1.0, bias=sig_bias[:])
         nc.scalar.activation(out=rest[:], in_=score_b[:], func=ACT.Sigmoid, bias=neg_sig_bias[:])
 
-        val_scales_g = gather("val_scales_g", val_scales, U8, offsets[:])
+        val_scales_g = gather("val_scales_g", val_scales, U8, offsets[:], tag="grouped_q2")
+        val_g = gather("val_g", val_words, U32, offsets[:])
         quantise("q", nc.vector.tensor_copy)
         score_a = psum.tile([P, SLOTS], F32, name="score_a")
         product(score_a, "q", key_g, key_scales_g[:])
         exp_bias = held.tile([P, 1], F32, name="exp_bias")
-        nc.gpsimd.tensor_scalar(exp_bias[:], ln_floor[:], l1_col[:], -1.0, ALU.add, ALU.mult)
+        nc.gpsimd.tensor_scalar(exp_bias[:], l1_col[:], -1.0, 0.0, ALU.mult, ALU.add)
 
-        both = held.tile([P, SLOTS], F32, name="both")
+        both = held.tile([P, SLOTS], F32, name="both", tag="grouped_q", align_bytes=64)
         nc.vector.tensor_tensor(both[:], share[:], rest[:], ALU.mult)
-        weight = held.tile([P, SLOTS], F32, name="weight")
+        weight = held.tile([P, SLOTS], F32, name="weight", tag="val_words")
         nc.vector.tensor_tensor(
             weight[:].rearrange("p (n j) -> p n j", j=PACK),
             size_bank[:].rearrange("p j n -> p n j"),
@@ -150,20 +148,21 @@ def tile_attend_gpclippedratio_b_kernel(
             ALU.mult,
         )
         quantise("g", nc.scalar.copy)
-        joint = held.tile([P, SLOTS], F32, name="joint", tag="raw_g")
-        nc.scalar.activation(out=joint[:], in_=score_a[:], func=ACT.Exp, bias=exp_bias[:])
+        inv_floor = held.tile([P, 1], F32, name="inv_floor", tag="raw_g")
+        nc.scalar.activation(out=inv_floor[:], in_=ln_floor[:], func=ACT.Exp, scale=-1.0)
+        joint = held.tile([P, SLOTS], F32, name="joint")
+        for h in range(HALVES):
+            nc.scalar.activation(out=joint[:, cols(h)], in_=score_a[:, cols(h)], func=ACT.Exp, bias=exp_bias[:])
 
-        val_g = [gather("val_g%d" % h, val_words, U32, half_list(h)) for h in range(HALVES)]
-        c0 = [psum.tile([P, HALF], F32, name="c0_%d" % h) for h in range(HALVES)]
-        xc, v, vsq, g, y = [
-            [held.tile([P, HALF], F32, name="%s%d" % (n, h)) for h in range(HALVES)]
-            for n in ("xc", "v", "vsq", "g", "y")
+        c0 = psum.tile([P, SLOTS], F32, name="c0")
+        product(c0, "g", val_g, val_scales_g[VAL_ROW:P, :])
+        xc = held.tile([P, SLOTS], F32, name="xc")
+        nc.vector.tensor_tensor(xc[:], c0[:], weight[:], ALU.mult)
+        v, vsq, g, y = [
+            [held.tile([P, HALF], F32, name="%s%d" % (n, h)) for h in range(HALVES)] for n in ("v", "vsq", "g", "y")
         ]
         for h in range(HALVES):
-            product(c0[h], "g", val_g[h], val_scales_g[VAL_ROW:P, cols(h)])
-            nc.vector.tensor_tensor(xc[h][:], c0[h][:], weight[:, cols(h)], ALU.mult)
-        for h in range(HALVES):
-            nc.vector.tensor_tensor(v[h][:], xc[h][:], joint[:, cols(h)], ALU.mult)
+            nc.vector.scalar_tensor_tensor(v[h][:], xc[:, cols(h)], inv_floor[:], joint[:, cols(h)], ALU.mult, ALU.mult)
             nc.scalar.activation(out=vsq[h][:], in_=v[h][:], func=ACT.Square)
         for h in range(HALVES):
             nc.vector.scalar_tensor_tensor(g[h][:], share[:, cols(h)], 0.5, vsq[h][:], ALU.subtract, ALU.mult)

@@ -59,8 +59,8 @@ def tile_attend_gpclippedratio_b_kernel(
 
         nc.sync.dma_start(offsets[:], offs)
         load_scales(nc.sync, key_scales, keys_scales, 0)
-        nc.sync.dma_start(out=floor_col[:], in_=floor)
-        nc.sync.dma_start(out=size_cols[:], in_=size[0].rearrange("(p j) -> p j", j=PACK))
+        nc.scalar.dma_start(out=floor_col[:], in_=floor)
+        nc.scalar.dma_start(out=size_cols[:], in_=size[0].rearrange("(p j) -> p j", j=PACK))
         load_words(key_words, keys_words)
         nc.sync.dma_start(out=l2_col[:], in_=l2)
         load_rows("q2", query2)
@@ -109,63 +109,77 @@ def tile_attend_gpclippedratio_b_kernel(
         def cols(h):
             return slice(h * HALF, (h + 1) * HALF)
 
-        def product(bank, name, words, scales):
+        def product(bank, name, words, scales, start=True, stop=True):
             nc.tensor.matmul_mx(
                 out=bank[:],
                 lhsT=codes[name][:].bitcast(FP8X4),
                 lhsT_scale=planes[name][:],
-                rhs=words[:].bitcast(FP8X4),
+                rhs=words.bitcast(FP8X4),
                 rhs_scale=scales,
-                start=True,
-                stop=True,
+                start=start,
+                stop=stop,
             )
 
         key_scales_g = gather("key_scales_g", key_scales, U8, offsets[:])
         key_g = gather("key_g", key_words, U32, offsets[:])
         quantise("q2", nc.scalar.copy)
-        score_b = psum.tile([P, SLOTS], F32, name="score_b")
-        product(score_b, "q2", key_g, key_scales_g[:])
+        score_b = [psum.tile([P, HALF], F32, name="score_b%d" % h) for h in range(HALVES)]
+        for h in (1, 0):
+            product(score_b[h], "q2", key_g[:, cols(h)], key_scales_g[:, cols(h)])
+        score_a = [psum.tile([P, HALF], F32, name="score_a%d" % h) for h in range(HALVES)]
+        product(score_a[1], "q2", key_g[:, cols(1)], key_scales_g[:, cols(1)], stop=False)
         share = held.tile([P, SLOTS], F32, name="share")
-        rest = held.tile([P, SLOTS], F32, name="rest")
-        nc.scalar.activation(out=share[:], in_=score_b[:], func=ACT.Sigmoid, scale=-1.0, bias=sig_bias[:])
-        nc.scalar.activation(out=rest[:], in_=score_b[:], func=ACT.Sigmoid, bias=neg_sig_bias[:])
+        rest = held.tile([P, HALF], F32, name="rest")
+        both = [
+            held.tile([P, HALF], F32, name="both0", tag="raw_q"),
+            held.tile([P, HALF], F32, name="both1"),
+        ]
+        for h in (1, 0):
+            nc.scalar.activation(
+                out=share[:, cols(h)], in_=score_b[h][:], func=ACT.Sigmoid, scale=-1.0, bias=sig_bias[:]
+            )
+        nc.scalar.activation(out=both[1][:], in_=share[:, cols(1)], func=ACT.Square)
+        nc.scalar.activation(out=rest[:], in_=score_b[0][:], func=ACT.Sigmoid, bias=neg_sig_bias[:])
 
         val_scales_g = gather("val_scales_g", val_scales, U8, offsets[:], tag="grouped_q2")
         val_g = gather("val_g", val_words, U32, offsets[:])
         quantise("q", nc.vector.tensor_copy)
-        score_a = psum.tile([P, SLOTS], F32, name="score_a")
-        product(score_a, "q", key_g, key_scales_g[:])
-        exp_bias = held.tile([P, 1], F32, name="exp_bias")
-        nc.gpsimd.tensor_scalar(exp_bias[:], l1_col[:], -1.0, 0.0, ALU.mult, ALU.add)
+        product(score_a[1], "q", key_g[:, cols(1)], key_scales_g[:, cols(1)], start=False)
+        product(score_a[0], "q", key_g[:, cols(0)], key_scales_g[:, cols(0)])
+        exp_bias = [held.tile([P, 1], F32, name="exp_bias%d" % h) for h in range(HALVES)]
+        nc.gpsimd.tensor_scalar(exp_bias[0][:], l1_col[:], -1.0, 0.0, ALU.mult, ALU.add)
+        nc.gpsimd.tensor_scalar(exp_bias[1][:], l1_col[:], sig_bias[:], -1.0, ALU.add, ALU.mult)
 
-        both = held.tile([P, SLOTS], F32, name="both", tag="grouped_q", align_bytes=64)
-        nc.vector.tensor_tensor(both[:], share[:], rest[:], ALU.mult)
-        weight = held.tile([P, SLOTS], F32, name="weight", tag="val_words")
-        nc.vector.tensor_tensor(
-            weight[:].rearrange("p (n j) -> p n j", j=PACK),
-            size_bank[:].rearrange("p j n -> p n j"),
-            both[:].rearrange("p (n j) -> p n j", j=PACK),
-            ALU.mult,
-        )
+        nc.vector.tensor_tensor(both[0][:], share[:, cols(0)], rest[:], ALU.mult)
         quantise("g", nc.scalar.copy)
+        weight = held.tile([P, SLOTS], F32, name="weight", tag="val_words")
+        for h in (1, 0):
+            n0 = h * HALF // PACK
+            nc.vector.tensor_tensor(
+                weight[:, cols(h)].rearrange("p (n j) -> p n j", j=PACK),
+                size_bank[:, :, n0 : n0 + HALF // PACK].rearrange("p j n -> p n j"),
+                both[h][:].rearrange("p (n j) -> p n j", j=PACK),
+                ALU.mult,
+            )
         inv_floor = held.tile([P, 1], F32, name="inv_floor", tag="raw_g")
         nc.scalar.activation(out=inv_floor[:], in_=ln_floor[:], func=ACT.Exp, scale=-1.0)
         joint = held.tile([P, SLOTS], F32, name="joint")
-        for h in range(HALVES):
-            nc.scalar.activation(out=joint[:, cols(h)], in_=score_a[:, cols(h)], func=ACT.Exp, bias=exp_bias[:])
+        for h in (1, 0):
+            nc.scalar.activation(out=joint[:, cols(h)], in_=score_a[h][:], func=ACT.Exp, bias=exp_bias[h][:])
 
-        c0 = psum.tile([P, SLOTS], F32, name="c0")
-        product(c0, "g", val_g, val_scales_g[VAL_ROW:P, :])
+        c0 = [psum.tile([P, HALF], F32, name="c0_%d" % h) for h in range(HALVES)]
         xc = held.tile([P, SLOTS], F32, name="xc")
-        nc.vector.tensor_tensor(xc[:], c0[:], weight[:], ALU.mult)
+        for h in (1, 0):
+            product(c0[h], "g", val_g[:, cols(h)], val_scales_g[VAL_ROW:P, cols(h)])
+            nc.vector.tensor_tensor(xc[:, cols(h)], c0[h][:], weight[:, cols(h)], ALU.mult)
         v, vsq, g, y = [
             [held.tile([P, HALF], F32, name="%s%d" % (n, h)) for h in range(HALVES)] for n in ("v", "vsq", "g", "y")
         ]
-        for h in range(HALVES):
+        for h in (1, 0):
             nc.vector.scalar_tensor_tensor(v[h][:], xc[:, cols(h)], inv_floor[:], joint[:, cols(h)], ALU.mult, ALU.mult)
             nc.scalar.activation(out=vsq[h][:], in_=v[h][:], func=ACT.Square)
-        for h in range(HALVES):
+        for h in (1, 0):
             nc.vector.scalar_tensor_tensor(g[h][:], share[:, cols(h)], 0.5, vsq[h][:], ALU.subtract, ALU.mult)
-        for h in range(HALVES):
+        for h in (1, 0):
             nc.vector.scalar_tensor_tensor(y[h][:], g[h][:], 64.0, base_sb[:, cols(h)], ALU.mult, ALU.add)
             nc.sync.dma_start(out=out[:, cols(h)], in_=y[h][:])

import concourse.mybir as mybir
from concourse.masks import make_identity

F32 = mybir.dt.float32
BF16 = mybir.dt.bfloat16
I32 = mybir.dt.int32
U32 = mybir.dt.uint32
U16 = mybir.dt.uint16
U8 = mybir.dt.uint8
FP8X4 = mybir.dt.float8_e4m3fn_x4
ACT = mybir.ActivationFunctionType
ALU = mybir.AluOpType

P = 128
PACK = 4
D, T, SLOTS, Q = 512, 2048, 512, 128
HALVES = 2
HALF = SLOTS // HALVES
VAL_ROW = 4

FLOPS = 3 * 2 * D * Q * SLOTS


def tile_attend_gpclippedratio_b_kernel(
    tc, query, query2, keys_words, keys_scales, l1, l2, floor, gout, vals_words, vals_scales, size, base, offs, out
):
    nc = tc.nc
    with (
        tc.tile_pool(name="held", bufs=1) as held,
        tc.psum_pool(name="psum", bufs=1) as psum,
    ):
        offsets = held.tile([P, SLOTS // 16], U16, name="offsets")
        key_words = held.tile([P, T], U32, name="key_words")
        val_words = held.tile([P, T], U32, name="val_words", tag="val_words")
        key_scales = held.tile([P, T], U8, name="key_scales")
        val_scales = held.tile([P, T], U8, name="val_scales")
        raw = {n: held.tile([P, PACK, Q], F32, name="raw_" + n, tag="raw_" + n) for n in ("q2", "q", "g")}
        floor_col = held.tile([P, 1], F32, name="floor_col")
        l1_col = held.tile([P, 1], F32, name="l1_col")
        l2_col = held.tile([P, 1], F32, name="l2_col")
        size_cols = held.tile([P, PACK], F32, name="size_cols")
        base_sb = held.tile([P, SLOTS], F32, name="base_sb")

        nc.gpsimd.memset(key_scales[:].bitcast(I32), 0)
        nc.vector.memset(val_scales[:].bitcast(I32), 0)

        def load_rows(name, src):
            nc.sync.dma_start(out=raw[name][:], in_=src.rearrange("(p j) w -> p j w", j=PACK))

        def load_words(dst, src):
            nc.sync.dma_start(out=dst[:].bitcast(I32), in_=src[0].rearrange("p n t -> p (n t)").bitcast(I32))

        def load_scales(queue, dst, src, first_row):
            for quad in range(4):
                queue.dma_start(
                    out=dst[32 * quad + first_row : 32 * quad + first_row + 4, :].bitcast(I32),
                    in_=src[0, 4 * quad : 4 * quad + 4, :].bitcast(I32),
                )

        nc.sync.dma_start(offsets[:], offs)
        load_scales(nc.sync, key_scales, keys_scales, 0)
        nc.scalar.dma_start(out=floor_col[:], in_=floor)
        nc.scalar.dma_start(out=size_cols[:], in_=size[0].rearrange("(p j) -> p j", j=PACK))
        load_words(key_words, keys_words)
        nc.sync.dma_start(out=l2_col[:], in_=l2)
        load_rows("q2", query2)
        load_scales(nc.sync, val_scales, vals_scales, VAL_ROW)
        load_words(val_words, vals_words)
        load_rows("g", gout)
        load_rows("q", query)
        nc.sync.dma_start(out=l1_col[:], in_=l1)
        nc.sync.dma_start(out=base_sb[:], in_=base)

        ident = held.tile([P, P], F32, name="ident")
        make_identity(nc, ident[:])

        size_bank = psum.tile([P, PACK, P], F32, name="size_bank")
        for j in range(PACK):
            nc.tensor.transpose(size_bank[:, j, :], size_cols[:, j : j + 1].to_broadcast([P, P]), ident[:])

        ln_floor = held.tile([P, 1], F32, name="ln_floor")
        nc.scalar.activation(out=ln_floor[:], in_=floor_col[:], func=ACT.Ln)
        warm = held.tile([P, 1], F32, name="warm")
        nc.scalar.activation(out=warm[:], in_=ln_floor[:], func=ACT.Sigmoid)
        sig_bias = held.tile([P, 1], F32, name="sig_bias")
        nc.scalar.activation(out=sig_bias[:], in_=ln_floor[:], func=ACT.Identity, bias=l2_col[:])
        neg_sig_bias = held.tile([P, 1], F32, name="neg_sig_bias", tag="grouped_g", align_bytes=64)
        nc.scalar.activation(out=neg_sig_bias[:], in_=sig_bias[:], func=ACT.Identity, scale=-1.0)

        codes, planes = {}, {}

        def quantise(name, copy):
            grouped = held.tile([P, Q, PACK], BF16, name="grouped_" + name, tag="grouped_" + name, align_bytes=64)
            copy(
                out=grouped[:].rearrange("p (c i) t -> p c t i", i=4),
                in_=raw[name][:].rearrange("p t (c i) -> p c t i", i=4),
            )
            codes[name] = held.tile([P, Q], U32, name="codes_" + name, align_bytes=64)
            planes[name] = held.tile([P, Q], U8, name="plane_" + name, align_bytes=64)
            nc.vector.quantize_mx(
                out=codes[name][:].bitcast(FP8X4), scales=planes[name][:], in_=grouped[:].rearrange("p w j -> p (w j)")
            )

        def gather(name, window, dtype, lists, tag=None):
            picked = held.tile([P, lists.shape[1] * 16], dtype, name=name, tag=tag or name, align_bytes=64)
            nc.vector.tensor_copy(picked[:], window[:].indirect(lists))
            return picked

        def cols(h):
            return slice(h * HALF, (h + 1) * HALF)

        def product(bank, name, words, scales, start=True, stop=True):
            nc.tensor.matmul_mx(
                out=bank[:],
                lhsT=codes[name][:].bitcast(FP8X4),
                lhsT_scale=planes[name][:],
                rhs=words.bitcast(FP8X4),
                rhs_scale=scales,
                start=start,
                stop=stop,
            )

        key_scales_g = gather("key_scales_g", key_scales, U8, offsets[:])
        key_g = gather("key_g", key_words, U32, offsets[:])
        quantise("q2", nc.scalar.copy)
        score_b = [psum.tile([P, HALF], F32, name="score_b%d" % h) for h in range(HALVES)]
        for h in (1, 0):
            product(score_b[h], "q2", key_g[:, cols(h)], key_scales_g[:, cols(h)])
        score_a = [psum.tile([P, HALF], F32, name="score_a%d" % h) for h in range(HALVES)]
        product(score_a[1], "q2", key_g[:, cols(1)], key_scales_g[:, cols(1)], stop=False)
        share = held.tile([P, SLOTS], F32, name="share")
        rest = held.tile([P, HALF], F32, name="rest")
        both = [
            held.tile([P, HALF], F32, name="both0", tag="raw_q"),
            held.tile([P, HALF], F32, name="both1"),
        ]
        for h in (1, 0):
            nc.scalar.activation(
                out=share[:, cols(h)], in_=score_b[h][:], func=ACT.Sigmoid, scale=-1.0, bias=sig_bias[:]
            )
        nc.scalar.activation(out=both[1][:], in_=share[:, cols(1)], func=ACT.Square)
        nc.scalar.activation(out=rest[:], in_=score_b[0][:], func=ACT.Sigmoid, bias=neg_sig_bias[:])

        val_scales_g = gather("val_scales_g", val_scales, U8, offsets[:], tag="grouped_q2")
        val_g = gather("val_g", val_words, U32, offsets[:])
        quantise("q", nc.vector.tensor_copy)
        product(score_a[1], "q", key_g[:, cols(1)], key_scales_g[:, cols(1)], start=False)
        product(score_a[0], "q", key_g[:, cols(0)], key_scales_g[:, cols(0)])
        exp_bias = [held.tile([P, 1], F32, name="exp_bias%d" % h) for h in range(HALVES)]
        nc.gpsimd.tensor_scalar(exp_bias[0][:], l1_col[:], -1.0, 0.0, ALU.mult, ALU.add)
        nc.gpsimd.tensor_scalar(exp_bias[1][:], l1_col[:], sig_bias[:], -1.0, ALU.add, ALU.mult)

        nc.vector.tensor_tensor(both[0][:], share[:, cols(0)], rest[:], ALU.mult)
        quantise("g", nc.scalar.copy)
        weight = held.tile([P, SLOTS], F32, name="weight", tag="val_words")
        for h in (1, 0):
            n0 = h * HALF // PACK
            nc.vector.tensor_tensor(
                weight[:, cols(h)].rearrange("p (n j) -> p n j", j=PACK),
                size_bank[:, :, n0 : n0 + HALF // PACK].rearrange("p j n -> p n j"),
                both[h][:].rearrange("p (n j) -> p n j", j=PACK),
                ALU.mult,
            )
        inv_floor = held.tile([P, 1], F32, name="inv_floor", tag="raw_g")
        nc.scalar.activation(out=inv_floor[:], in_=ln_floor[:], func=ACT.Exp, scale=-1.0)
        joint = held.tile([P, SLOTS], F32, name="joint")
        for h in (1, 0):
            nc.scalar.activation(out=joint[:, cols(h)], in_=score_a[h][:], func=ACT.Exp, bias=exp_bias[h][:])

        c0 = [psum.tile([P, HALF], F32, name="c0_%d" % h) for h in range(HALVES)]
        xc = held.tile([P, SLOTS], F32, name="xc")
        for h in (1, 0):
            product(c0[h], "g", val_g[:, cols(h)], val_scales_g[VAL_ROW:P, cols(h)])
            nc.vector.tensor_tensor(xc[:, cols(h)], c0[h][:], weight[:, cols(h)], ALU.mult)
        v, vsq, g, y = [
            [held.tile([P, HALF], F32, name="%s%d" % (n, h)) for h in range(HALVES)] for n in ("v", "vsq", "g", "y")
        ]
        for h in (1, 0):
            nc.vector.scalar_tensor_tensor(v[h][:], xc[:, cols(h)], inv_floor[:], joint[:, cols(h)], ALU.mult, ALU.mult)
            nc.scalar.activation(out=vsq[h][:], in_=v[h][:], func=ACT.Square)
        for h in (1, 0):
            nc.vector.scalar_tensor_tensor(g[h][:], share[:, cols(h)], 0.5, vsq[h][:], ALU.subtract, ALU.mult)
        for h in (1, 0):
            nc.vector.scalar_tensor_tensor(y[h][:], g[h][:], 64.0, base_sb[:, cols(h)], ALU.mult, ALU.add)
            nc.sync.dma_start(out=out[:, cols(h)], in_=y[h][:])
